import numpy as np
import ml_dtypes


def mxq(x, axis, fmt="e4m3"):
    dtype, down = {"e4m3": (ml_dtypes.float8_e4m3fn, 7), "e5m2": (ml_dtypes.float8_e5m2, 14)}[fmt]
    v = np.moveaxis(np.asarray(x, np.float32).astype(ml_dtypes.bfloat16).astype(np.float64), axis, -1)
    blocks = v.reshape(v.shape[:-1] + (-1, 32))
    amax = np.abs(blocks).max(-1, keepdims=True)
    byte = np.maximum(np.where(amax > 0, np.frexp(amax)[1] - 1 + 127, 0) - down, 1)
    scale = np.exp2(byte - 127.0)
    codes = (blocks / scale).astype(np.float32).astype(dtype).astype(np.float64)
    return np.moveaxis((codes * scale).reshape(v.shape), -1, axis)


WIDE = False


def mx_kscale(k):
    if not WIDE:
        return np.ones(k)
    levels = np.array([10, -10, 5, -5, 0])
    if k % 512:
        return np.exp2(np.random.permutation(np.resize(levels, k // 32))).repeat(32)
    a = np.empty((k // 512, 16))
    for p in range(k // 512):
        a[p, :8] = np.random.permutation(np.resize(levels, 8))
        for g in range(8):
            far = levels[np.abs(levels - a[p, g]) >= 10]
            a[p, g + 8] = far[np.random.randint(len(far))]
    return np.exp2(a.ravel()).repeat(32)


def f64(x):
    return np.asarray(x).astype(np.float64)


def striped(idx):
    return np.tile(np.asarray(idx).reshape(-1, 16).T, (8, 1)).astype(np.uint16)


def unstriped(offs):
    return offs[:16].T.reshape(-1).astype(np.int64)


E2M1 = np.array([0.0, 0.5, 1.0, 1.5, 2.0, 3.0, 4.0, 6.0, -0.0, -0.5, -1.0, -1.5, -2.0, -3.0, -4.0, -6.0])


def pack_weight(w, fmt):
    k, n = w.shape
    w = f64(np.asarray(w, np.float32).astype(ml_dtypes.bfloat16)).reshape(k // 32, 32, n)
    amax = np.abs(w).max(1)
    if fmt == "e4m3":
        byte = np.frexp(amax)[1] - 1 + 127 - 7
    else:
        mant, ex = np.frexp(amax / 6.0)
        byte = np.where(mant > 0.5, ex, ex - 1) + 127
    byte = np.clip(np.where(amax > 0, byte, 1), 1, 254)
    scaled = (w * np.exp2(127.0 - byte)[:, None, :]).reshape(k, n).astype(np.float32)
    by_word = np.ascontiguousarray(scaled.reshape(k // 512, 128, 4, n).transpose(0, 1, 3, 2))
    if fmt == "e4m3":
        words = by_word.astype(ml_dtypes.float8_e4m3fn).view(np.uint8)
    else:
        c = by_word.astype(ml_dtypes.float4_e2m1fn).view(np.uint8) & 0xF
        words = (c[..., 0::2] | (c[..., 1::2] << 4)).reshape(k // 512, 128, 2 * n)
    return np.ascontiguousarray(words), np.ascontiguousarray(byte.astype(np.uint8).reshape(k // 512, 16, n))


def unpack_weight(words, scales, fmt):
    g, _, n = scales.shape
    words = np.ascontiguousarray(words).reshape(g, 128, n, -1)
    if fmt == "e4m3":
        vals = words.view(ml_dtypes.float8_e4m3fn).astype(np.float64)
    else:
        nib = np.empty((g, 128, n, 4), np.uint8)
        nib[..., 0::2] = words & 0xF
        nib[..., 1::2] = words >> 4
        vals = E2M1[nib]
    vals = vals * np.repeat(np.exp2(scales.astype(np.float64) - 127.0), 8, axis=1)[..., None]
    return vals.transpose(0, 1, 3, 2).reshape(g * 512, n)


D, T, U, I, J, G = 512, 1024, 1024, 256, 512, 32


def setup_inputs():
    n = np.random.standard_normal
    idx = np.random.permutation(T)[:I]
    idx2 = np.random.permutation(U)[:J]
    fd = mx_kscale(D)
    tabbp = pack_weight(n((D, U)) / fd[:, None], "e2m1")
    return {
        "taba": (n((D, T)) * 1 / np.sqrt(D) * fd[:, None]).astype(np.float32),
        "dtab": (n((D, T)) * 1.3 / np.sqrt(D) * fd[:, None]).astype(np.float32),
        "tabb_words": tabbp[0],
        "tabb_scales": tabbp[1],
        "pw": (np.random.uniform(0.5, 2.0, (1, J))).astype(np.float32),
        "base": (0.3 * n((I, J))).astype(np.float32),
        "offs": striped(idx),
        "offs2": striped(idx2),
    }


def reference(taba, dtab, tabb_words, tabb_scales, pw, base, offs, offs2):
    idx = unstriped(offs)
    idx2 = unstriped(offs2)
    tabbu = unpack_weight(tabb_words, tabb_scales, "e2m1")
    tabaidxq = mxq(f64(taba)[:, idx], 0, "e4m3")
    tabbidx2g = tabbu[:, idx2]
    s = tabaidxq.T @ tabbidx2g
    dtabidxq = mxq(f64(dtab)[:, idx], 0, "e4m3")
    ts = dtabidxq.T @ tabbidx2g
    h1 = np.tanh(s)
    m1 = h1.reshape(I, G, J // G).mean(axis=2)
    mr = np.repeat(m1, J // G, axis=1)
    dmr = f64(pw) * (h1 - mr) * 2.0 * (-1.0)
    dm1 = dmr.reshape(I, G, J // G).sum(axis=2)
    e1 = dm1 / 16.0
    r1 = np.repeat(e1, J // G, axis=1)
    dh1 = f64(pw) * (h1 - mr) * 2.0 + r1
    xh1 = ts * (1.0 - np.square(h1))
    xm1 = xh1.reshape(I, G, J // G).mean(axis=2)
    xmr = np.repeat(xm1, J // G, axis=1)
    xdmr = (xh1 - xmr) * f64(pw) * 2.0 * (-1.0)
    xdm1 = xdmr.reshape(I, G, J // G).sum(axis=2)
    xe1 = xdm1 / 16.0
    xr1 = np.repeat(xe1, J // G, axis=1)
    xdh1 = (xh1 - xmr) * f64(pw) * 2.0 + xr1
    xds = xdh1 * (1.0 - np.square(h1)) + xh1 * h1 * 2.0 * (-1.0) * dh1
    y = xds + f64(base)
    return y

@@ -1,0 +1,266 @@
+from contextlib import ExitStack
+
+import concourse.mybir as mybir
+from concourse.masks import make_identity
+
+D, T, U, I, J, G = 512, 1024, 1024, 256, 512, 32
+FLOPS = 2 * 2 * D * I * J
+
+F32 = mybir.dt.float32
+BF16 = mybir.dt.bfloat16
+I32 = mybir.dt.int32
+U32 = mybir.dt.uint32
+U16 = mybir.dt.uint16
+U8 = mybir.dt.uint8
+FP8X4 = mybir.dt.float8_e4m3fn_x4
+FP4X4 = mybir.dt.float4_e2m1fn_x4
+ALU = mybir.AluOpType
+ACT = mybir.ActivationFunctionType
+AX = mybir.AxisListType
+
+P = 128
+PACK = 4
+HALVES = I // P
+JT = J // P
+GROUP = J // G
+
+
+def tile_attend_hvpairbalance_kernel(tc, taba, dtab, tabb_words, tabb_scales, pw, base, offs, offs2, out):
+    nc = tc.nc
+    with ExitStack() as ctx:
+        sb = ctx.enter_context(tc.tile_pool(name="sb", bufs=1))
+        ps = ctx.enter_context(tc.psum_pool(name="ps", bufs=1))
+
+        def new(name, shape, dtype, align=64):
+            return sb.tile(shape, dtype, name=name, align_bytes=align)
+
+        list_i = new("list_i", [P, I // 16], U16)
+        list_j = new("list_j", [P, J // 16], U16)
+        words = new("words", [P, U], U16)
+        scales = new("scales", [P, U], U8)
+        w16 = new("w16", [P, GROUP], F32)
+        planes_a = [new("plane_a%d" % t, [P, T], F32) for t in range(PACK)]
+        planes_d = [new("plane_d%d" % t, [P, T], F32) for t in range(PACK)]
+        base_sb = [new("base%d" % h, [P, J], F32) for h in range(HALVES)]
+        ident = new("ident", [P, P], F32)
+        warm = new("warm", [P, 1], F32)
+        warm_out = new("warm_out", [P, 1], F32)
+
+        nc.gpsimd.memset(scales[:].bitcast(I32), 0)
+        nc.gpsimd.memset(warm[:], 0.0)
+        nc.scalar.activation(warm_out[:], warm[:], ACT.Tanh)
+        make_identity(nc, ident[:])
+
+        a_rows = taba.rearrange("(p t) c -> t p c", t=PACK)
+        d_rows = dtab.rearrange("(p t) c -> t p c", t=PACK)
+        nc.sync.dma_start(list_j[:], offs2)
+        nc.sync.dma_start(words[:].bitcast(I32), tabb_words[0].bitcast(I32))
+        nc.sync.dma_start(planes_a[0][:], a_rows[0])
+        nc.sync.dma_start(list_i[:], offs)
+        for r in range(4):
+            nc.scalar.dma_start(scales[r:P:32, :].bitcast(I32), tabb_scales[0, r:16:4, :].bitcast(I32))
+        nc.sync.dma_start(planes_a[1][:], a_rows[1])
+        nc.scalar.dma_start(w16[:], pw.rearrange("o (g r) -> g o r", r=GROUP).to_broadcast([G, 4, GROUP]))
+        for t in range(2, PACK):
+            nc.sync.dma_start(planes_a[t][:], a_rows[t])
+        for t in range(PACK):
+            nc.sync.dma_start(planes_d[t][:], d_rows[t])
+        for h in range(HALVES):
+            nc.sync.dma_start(base_sb[h][:], base[h * P : (h + 1) * P, :])
+
+        lane = new("lane", [P, 4], F32)
+        nc.vector.tensor_reduce(lane[:], ident[:].rearrange("p (a c) -> p c a", c=4), AX.X, ALU.add)
+
+        words_g = new("words_g", [P, J], U16)
+        scales_g = new("scales_g", [P, J], U8)
+        words_t = new("words_t", [P, JT, P], U16)
+        scales_t = new("scales_t", [P, JT, P], U8)
+        nc.vector.tensor_copy(words_g[:], words[:].indirect(list_j[:]))
+        nc.vector.tensor_copy(scales_g[:], scales[:].indirect(list_j[:]))
+        nc.vector.tensor_copy(
+            words_t[:].bitcast(I32).rearrange("p t (g e) -> p t g e", e=2),
+            words_g[:].bitcast(I32).rearrange("p (g t e) -> p t g e", t=JT, e=2),
+        )
+        nc.vector.tensor_copy(
+            scales_t[:].bitcast(I32),
+            scales_g[:].bitcast(I32).rearrange("p (g t) -> p t g", t=JT),
+        )
+
+        picked = new("picked", [P, JT, 4], F32)
+        w4 = new("w4", [P, JT], F32)
+        wsum = new("wsum", [P, 1], F32)
+        wmean_neg = new("wmean_neg", [P, 1], F32)
+        w_n8 = new("w_n8", [P, JT], F32)
+        w_6 = new("w_6", [P, JT], F32)
+        w_n2 = new("w_n2", [P, JT], F32)
+        wc_n8 = new("wc_n8", [P, JT], F32)
+        wc_p8 = new("wc_p8", [P, JT], F32)
+        nc.gpsimd.tensor_tensor(
+            picked[:], w16[:].rearrange("p (t c) -> p t c", c=4), lane[:].unsqueeze(1).to_broadcast([P, JT, 4]), ALU.mult
+        )
+        nc.vector.tensor_reduce(w4[:], picked[:], AX.X, ALU.add)
+        nc.vector.tensor_reduce(wsum[:], w16[:], AX.X, ALU.add)
+        nc.gpsimd.tensor_scalar(wmean_neg[:], wsum[:], -1.0 / GROUP, 0.0, ALU.mult, ALU.add)
+        nc.gpsimd.tensor_scalar(w_n8[:], w4[:], -0.125, 0.0, ALU.mult, ALU.add)
+        nc.gpsimd.tensor_scalar(wc_n8[:], w4[:], wmean_neg[:], -0.125, ALU.add, ALU.mult)
+        nc.gpsimd.tensor_scalar(w_6[:], w4[:], 6.0, 0.0, ALU.mult, ALU.add)
+        nc.gpsimd.tensor_scalar(w_n2[:], w4[:], -2.0, 0.0, ALU.mult, ALU.add)
+        nc.gpsimd.tensor_scalar(wc_p8[:], w4[:], wmean_neg[:], 0.125, ALU.add, ALU.mult)
+
+        def gather_plane(woven, planes, t):
+            nc.vector.tensor_copy(woven[:, :, t], planes[t][:].indirect(list_i[:]))
+
+        def gather_plane_half(woven, planes, t, h):
+            cols = P // 16
+            nc.vector.tensor_copy(woven[:, h * P : (h + 1) * P, t], planes[t][:].indirect(list_i[:, h * cols : (h + 1) * cols]))
+
+        def quantize(name, woven, h):
+            codes = new("codes_%s%d" % (name, h), [P, P], U32)
+            plane = new("sc_%s%d" % (name, h), [P, P], U8)
+            nc.vector.quantize_mx(
+                out=codes[:].bitcast(FP8X4), scales=plane[:], in_=woven[:, h * P : (h + 1) * P, :].rearrange("p c t -> p (c t)")
+            )
+            return codes, plane
+
+        def scores(bank, quantized):
+            codes, plane = quantized
+            for t in range(JT):
+                nc.tensor.matmul_mx(
+                    out=bank[:, t, :],
+                    lhsT=words_t[:, t, :].bitcast(FP4X4),
+                    lhsT_scale=scales_t[:, t, :],
+                    rhs=codes[:].bitcast(FP8X4),
+                    rhs_scale=plane[:],
+                    start=True,
+                    stop=True,
+                )
+
+        def turn(dst, src, start, stop):
+            nc.tensor.matmul(dst, src, ident[:], start=start, stop=stop, is_transpose=True)
+
+        def sum_over_tiles(dst, src):
+            for t in range(JT):
+                turn(dst, src[:, t, :], t == 0, t == JT - 1)
+
+        def per_tile(dst, src, scale, bias=None):
+            for t in range(JT):
+                if bias is None:
+                    nc.scalar.activation(dst[:, t, :], src[:, t, :], ACT.Copy, scale=scale[:, t : t + 1])
+                else:
+                    nc.scalar.activation(
+                        dst[:, t, :], src[:, t, :], ACT.Identity, bias=bias[:, t : t + 1], scale=scale[:, t : t + 1]
+                    )
+
+        def group_reduce(name, bank):
+            red = new("red_" + name, [P, 2 * G, 1], F32)
+            nc.vector.tensor_reduce(red[:], bank[:, 0:2, :].rearrange("p q (g c) -> p (q g) c", c=4), AX.X, ALU.add)
+            return red
+
+        def group_spread(name, bank, red):
+            rep = new("rep_" + name, [P, 2 * G, 4], F32)
+            nc.vector.tensor_copy(rep[:], red[:].to_broadcast([P, 2 * G, 4]))
+            flat = rep[:].rearrange("p (q g) c -> p q (g c)", q=2)
+            for q in range(2):
+                turn(bank[:, 2 + q, :], flat[:, q, :], True, True)
+
+        big = [P, JT, P]
+        halves = range(HALVES)
+        woven_a = new("woven_a", [P, I, PACK], BF16)
+        woven_d = new("woven_d", [P, I, PACK], BF16)
+        for t in range(PACK - 1):
+            gather_plane(woven_a, planes_a, t)
+        for h in halves:
+            gather_plane_half(woven_a, planes_a, PACK - 1, h)
+        quant_a = [quantize("a", woven_a, h) for h in halves]
+        s_bank = [ps.tile(big, F32, name="s%d" % h, tag="sy%d" % h) for h in halves]
+        for h in halves:
+            scores(s_bank[h], quant_a[h])
+
+        th = [new("th%d" % h, big, F32) for h in halves]
+        wth = [new("wth%d" % h, big, F32) for h in halves]
+        th2 = [new("thsq%d" % h, big, F32) for h in halves]
+        h_bank = [ps.tile(big, F32, name="hb%d" % h) for h in halves]
+        for h in halves:
+            nc.scalar.activation(th[h][:], s_bank[h][:], ACT.Tanh)
+            per_tile(wth[h], th[h], w_n8)
+            sum_over_tiles(h_bank[h][:, 0, :], th[h])
+            sum_over_tiles(h_bank[h][:, 1, :], wth[h])
+        for h in halves:
+            nc.scalar.activation(th2[h][:], th[h][:], ACT.Square)
+
+        for t in range(PACK - 1):
+            gather_plane(woven_d, planes_d, t)
+        red_h = [group_reduce("h%d" % h, h_bank[h]) for h in halves]
+        for h in halves:
+            group_spread("h%d" % h, h_bank[h], red_h[h])
+        for h in halves:
+            gather_plane_half(woven_d, planes_d, PACK - 1, h)
+        quant_d = [quantize("d", woven_d, h) for h in halves]
+        ts_bank = [ps.tile(big, F32, name="ts%d" % h) for h in halves]
+        for h in halves:
+            scores(ts_bank[h], quant_d[h])
+
+        ph = [new("ph%d" % h, [P, P], F32) for h in halves]
+        rh = [new("rh%d" % h, big, F32) for h in halves]
+        for h in halves:
+            nc.scalar.copy(ph[h][:], h_bank[h][:, 3, :])
+            for t in range(JT):
+                nc.vector.scalar_tensor_tensor(
+                    rh[h][:, t, :], h_bank[h][:, 2, :], wc_n8[:, t : t + 1], ph[h][:], ALU.mult, ALU.add
+                )
+
+        def flat(x):
+            return x[:].rearrange("p t i -> p (t i)")
+
+        x = [new("x%d" % h, big, F32) for h in halves]
+        wx = [new("wx%d" % h, big, F32) for h in halves]
+        x_bank = [ps.tile(big, F32, name="xb%d" % h) for h in halves]
+        for h in halves:
+            nc.vector.scalar_tensor_tensor(flat(x[h]), flat(th2[h]), 1.0, flat(ts_bank[h]), ALU.subtract, ALU.mult)
+            per_tile(wx[h], x[h], w_n8)
+            sum_over_tiles(x_bank[h][:, 0, :], x[h])
+            sum_over_tiles(x_bank[h][:, 1, :], wx[h])
+
+        e = [new("e%d" % h, big, F32) for h in halves]
+        g = [new("g%d" % h, big, F32) for h in halves]
+        a = [new("a%d" % h, big, F32) for h in halves]
+        b = [new("b%d" % h, big, F32) for h in halves]
+        z = [new("z%d" % h, big, F32) for h in halves]
+        for h in halves:
+            per_tile(e[h], th2[h], w_6, w_n2)
+        for h in halves:
+            per_tile(b[h], th2[h], wc_n8, wc_p8)
+        for h in halves:
+            nc.vector.scalar_tensor_tensor(flat(g[h]), flat(th[h]), 2.0, flat(rh[h]), ALU.mult, ALU.mult)
+        red_x = [group_reduce("x%d" % h, x_bank[h]) for h in halves]
+        for h in halves:
+            group_spread("x%d" % h, x_bank[h], red_x[h])
+        for h in halves:
+            nc.vector.tensor_tensor(flat(a[h]), flat(g[h]), flat(e[h]), ALU.add)
+        for h in halves:
+            nc.vector.tensor_tensor(flat(z[h]), flat(a[h]), flat(x[h]), ALU.mult)
+
+        bm = [new("bm%d" % h, big, F32) for h in halves]
+        up = [new("up%d" % h, big, F32) for h in halves]
+        y_bank = [ps.tile(big, F32, name="y%d" % h, tag="sy%d" % h) for h in halves]
+        y = [new("yo%d" % h, [P, J], F32) for h in halves]
+        for h in halves:
+            for t in range(JT):
+                turn(y_bank[h][:, t, :], z[h][:, t, :], t == 0, False)
+        for h in halves:
+            nc.vector.tensor_tensor(bm[h][:], x_bank[h][:, 2:3, :].to_broadcast(big), b[h][:], ALU.mult)
+            nc.vector.scalar_tensor_tensor(
+                up[h][:], th2[h][:], 1.0, x_bank[h][:, 3:4, :].to_broadcast(big), ALU.subtract, ALU.mult
+            )
+            for t in range(JT):
+                turn(y_bank[h][:, t, :], bm[h][:, t, :], False, False)
+            for t in range(JT):
+                turn(y_bank[h][:, t, :], up[h][:, t, :], False, t == JT - 1)
+        for h in halves:
+            nc.vector.tensor_tensor(
+                y[h][:].rearrange("i (g t c) -> i g t c", t=JT, c=4),
+                y_bank[h][:].rearrange("i t (g c) -> i g t c", c=4),
+                base_sb[h][:].rearrange("i (g t c) -> i g t c", t=JT, c=4),
+                ALU.add,
+            )
+            nc.sync.dma_start(out[h * P : (h + 1) * P, :], y[h][:])

@@ -31,8 +31,8 @@ def tile_attend_hvpairbalance_kernel(tc, taba, dtab, tabb_words, tabb_scales, pw
         sb = ctx.enter_context(tc.tile_pool(name="sb", bufs=1))
         ps = ctx.enter_context(tc.psum_pool(name="ps", bufs=1))
 
-        def new(name, shape, dtype, align=64):
-            return sb.tile(shape, dtype, name=name, align_bytes=align)
+        def new(name, shape, dtype, tag=None):
+            return sb.tile(shape, dtype, name=name, tag=tag or name, align_bytes=64)
 
         list_i = new("list_i", [P, I // 16], U16)
         list_j = new("list_j", [P, J // 16], U16)
@@ -46,21 +46,21 @@ def tile_attend_hvpairbalance_kernel(tc, taba, dtab, tabb_words, tabb_scales, pw
         warm = new("warm", [P, 1], F32)
         warm_out = new("warm_out", [P, 1], F32)
 
-        nc.gpsimd.memset(scales[:].bitcast(I32), 0)
+        nc.vector.memset(scales[:].bitcast(I32), 0)
         nc.gpsimd.memset(warm[:], 0.0)
         nc.scalar.activation(warm_out[:], warm[:], ACT.Tanh)
         make_identity(nc, ident[:])
 
         a_rows = taba.rearrange("(p t) c -> t p c", t=PACK)
         d_rows = dtab.rearrange("(p t) c -> t p c", t=PACK)
+        nc.gpsimd.dma_start(w16[:], pw.rearrange("o (g r) -> g o r", r=GROUP).to_broadcast([G, 4, GROUP]))
         nc.sync.dma_start(list_j[:], offs2)
         nc.sync.dma_start(words[:].bitcast(I32), tabb_words[0].bitcast(I32))
-        nc.sync.dma_start(planes_a[0][:], a_rows[0])
-        nc.sync.dma_start(list_i[:], offs)
         for r in range(4):
-            nc.scalar.dma_start(scales[r:P:32, :].bitcast(I32), tabb_scales[0, r:16:4, :].bitcast(I32))
+            nc.sync.dma_start(scales[r:P:32, :].bitcast(I32), tabb_scales[0, r:16:4, :].bitcast(I32))
+        nc.sync.dma_start(planes_a[0][:], a_rows[0])
         nc.sync.dma_start(planes_a[1][:], a_rows[1])
-        nc.scalar.dma_start(w16[:], pw.rearrange("o (g r) -> g o r", r=GROUP).to_broadcast([G, 4, GROUP]))
+        nc.sync.dma_start(list_i[:], offs)
         for t in range(2, PACK):
             nc.sync.dma_start(planes_a[t][:], a_rows[t])
         for t in range(PACK):
@@ -86,31 +86,31 @@ def tile_attend_hvpairbalance_kernel(tc, taba, dtab, tabb_words, tabb_scales, pw
             scales_g[:].bitcast(I32).rearrange("p (g t) -> p t g", t=JT),
         )
 
-        picked = new("picked", [P, JT, 4], F32)
+        picked = new("picked", [P, JT, 4], F32, "words")
         w4 = new("w4", [P, JT], F32)
-        wsum = new("wsum", [P, 1], F32)
-        wmean_neg = new("wmean_neg", [P, 1], F32)
+        wsum = new("wsum", [P, 1], F32, "words_g")
+        wmean_p8 = new("wmean_p8", [P, 1], F32)
         w_n8 = new("w_n8", [P, JT], F32)
         w_6 = new("w_6", [P, JT], F32)
         w_n2 = new("w_n2", [P, JT], F32)
         wc_n8 = new("wc_n8", [P, JT], F32)
         wc_p8 = new("wc_p8", [P, JT], F32)
-        nc.gpsimd.tensor_tensor(
+        nc.vector.tensor_tensor(
             picked[:], w16[:].rearrange("p (t c) -> p t c", c=4), lane[:].unsqueeze(1).to_broadcast([P, JT, 4]), ALU.mult
         )
-        nc.vector.tensor_reduce(w4[:], picked[:], AX.X, ALU.add)
         nc.vector.tensor_reduce(wsum[:], w16[:], AX.X, ALU.add)
-        nc.gpsimd.tensor_scalar(wmean_neg[:], wsum[:], -1.0 / GROUP, 0.0, ALU.mult, ALU.add)
-        nc.gpsimd.tensor_scalar(w_n8[:], w4[:], -0.125, 0.0, ALU.mult, ALU.add)
-        nc.gpsimd.tensor_scalar(wc_n8[:], w4[:], wmean_neg[:], -0.125, ALU.add, ALU.mult)
-        nc.gpsimd.tensor_scalar(w_6[:], w4[:], 6.0, 0.0, ALU.mult, ALU.add)
-        nc.gpsimd.tensor_scalar(w_n2[:], w4[:], -2.0, 0.0, ALU.mult, ALU.add)
-        nc.gpsimd.tensor_scalar(wc_p8[:], w4[:], wmean_neg[:], 0.125, ALU.add, ALU.mult)
+        nc.vector.tensor_reduce(w4[:], picked[:], AX.X, ALU.add)
+        nc.scalar.activation(wmean_p8[:], wsum[:], ACT.Copy, scale=0.125 / GROUP)
+        nc.scalar.activation(w_n8[:], w4[:], ACT.Copy, scale=-0.125)
+        nc.scalar.activation(wc_n8[:], w4[:], ACT.Identity, bias=wmean_p8[:], scale=-0.125)
+        nc.scalar.activation(w_6[:], w4[:], ACT.Copy, scale=6.0)
+        nc.scalar.activation(w_n2[:], w4[:], ACT.Copy, scale=-2.0)
+        nc.scalar.activation(wc_p8[:], wc_n8[:], ACT.Copy, scale=-1.0)
 
-        def gather_plane(woven, planes, t):
+        def gather_woven(woven, planes, t):
             nc.vector.tensor_copy(woven[:, :, t], planes[t][:].indirect(list_i[:]))
 
-        def gather_plane_half(woven, planes, t, h):
+        def gather_woven_half(woven, planes, t, h):
             cols = P // 16
             nc.vector.tensor_copy(woven[:, h * P : (h + 1) * P, t], planes[t][:].indirect(list_i[:, h * cols : (h + 1) * cols]))
 
@@ -151,14 +151,14 @@ def tile_attend_hvpairbalance_kernel(tc, taba, dtab, tabb_words, tabb_scales, pw
                         dst[:, t, :], src[:, t, :], ACT.Identity, bias=bias[:, t : t + 1], scale=scale[:, t : t + 1]
                     )
 
-        def group_reduce(name, bank):
-            red = new("red_" + name, [P, 2 * G, 1], F32)
+        def group_reduce(name, bank, tag=None):
+            red = new("red_" + name, [P, 2 * G, 1], F32, tag)
             nc.vector.tensor_reduce(red[:], bank[:, 0:2, :].rearrange("p q (g c) -> p (q g) c", c=4), AX.X, ALU.add)
             return red
 
-        def group_spread(name, bank, red):
+        def group_spread(name, bank, red, copy):
             rep = new("rep_" + name, [P, 2 * G, 4], F32)
-            nc.vector.tensor_copy(rep[:], red[:].to_broadcast([P, 2 * G, 4]))
+            copy(rep[:], red[:].to_broadcast([P, 2 * G, 4]))
             flat = rep[:].rearrange("p (q g) c -> p q (g c)", q=2)
             for q in range(2):
                 turn(bank[:, 2 + q, :], flat[:, q, :], True, True)
@@ -167,10 +167,13 @@ def tile_attend_hvpairbalance_kernel(tc, taba, dtab, tabb_words, tabb_scales, pw
         halves = range(HALVES)
         woven_a = new("woven_a", [P, I, PACK], BF16)
         woven_d = new("woven_d", [P, I, PACK], BF16)
-        for t in range(PACK - 1):
-            gather_plane(woven_a, planes_a, t)
+        dense_a = new("dense_a", [P, 2, I], BF16)
+        for t in range(2):
+            nc.vector.tensor_copy(dense_a[:, t, :], planes_a[t][:].indirect(list_i[:]))
+        nc.scalar.copy(woven_a[:, :, 0:2], dense_a[:].rearrange("p t c -> p c t"))
+        gather_woven(woven_a, planes_a, 2)
         for h in halves:
-            gather_plane_half(woven_a, planes_a, PACK - 1, h)
+            gather_woven_half(woven_a, planes_a, PACK - 1, h)
         quant_a = [quantize("a", woven_a, h) for h in halves]
         s_bank = [ps.tile(big, F32, name="s%d" % h, tag="sy%d" % h) for h in halves]
         for h in halves:
@@ -181,7 +184,8 @@ def tile_attend_hvpairbalance_kernel(tc, taba, dtab, tabb_words, tabb_scales, pw
         th2 = [new("thsq%d" % h, big, F32) for h in halves]
         h_bank = [ps.tile(big, F32, name="hb%d" % h) for h in halves]
         for h in halves:
-            nc.scalar.activation(th[h][:], s_bank[h][:], ACT.Tanh)
+            for pair in range(0, JT, 2):
+                nc.scalar.activation(th[h][:, pair : pair + 2, :], s_bank[h][:, pair : pair + 2, :], ACT.Tanh)
             per_tile(wth[h], th[h], w_n8)
             sum_over_tiles(h_bank[h][:, 0, :], th[h])
             sum_over_tiles(h_bank[h][:, 1, :], wth[h])
@@ -189,16 +193,16 @@ def tile_attend_hvpairbalance_kernel(tc, taba, dtab, tabb_words, tabb_scales, pw
             nc.scalar.activation(th2[h][:], th[h][:], ACT.Square)
 
         for t in range(PACK - 1):
-            gather_plane(woven_d, planes_d, t)
-        red_h = [group_reduce("h%d" % h, h_bank[h]) for h in halves]
+            gather_woven(woven_d, planes_d, t)
         for h in halves:
-            group_spread("h%d" % h, h_bank[h], red_h[h])
-        for h in halves:
-            gather_plane_half(woven_d, planes_d, PACK - 1, h)
+            gather_woven_half(woven_d, planes_d, PACK - 1, h)
         quant_d = [quantize("d", woven_d, h) for h in halves]
         ts_bank = [ps.tile(big, F32, name="ts%d" % h) for h in halves]
         for h in halves:
             scores(ts_bank[h], quant_d[h])
+        red_h = [group_reduce("h%d" % h, h_bank[h], ("plane_d3", "woven_d")[h]) for h in halves]
+        for h in halves:
+            group_spread("h%d" % h, h_bank[h], red_h[h], nc.scalar.copy)
 
         ph = [new("ph%d" % h, [P, P], F32) for h in halves]
         rh = [new("rh%d" % h, big, F32) for h in halves]
@@ -221,20 +225,20 @@ def tile_attend_hvpairbalance_kernel(tc, taba, dtab, tabb_words, tabb_scales, pw
             sum_over_tiles(x_bank[h][:, 0, :], x[h])
             sum_over_tiles(x_bank[h][:, 1, :], wx[h])
 
-        e = [new("e%d" % h, big, F32) for h in halves]
+        e = [new("e%d" % h, big, F32, "wx%d" % h) for h in halves]
         g = [new("g%d" % h, big, F32) for h in halves]
         a = [new("a%d" % h, big, F32) for h in halves]
-        b = [new("b%d" % h, big, F32) for h in halves]
         z = [new("z%d" % h, big, F32) for h in halves]
         for h in halves:
             per_tile(e[h], th2[h], w_6, w_n2)
         for h in halves:
-            per_tile(b[h], th2[h], wc_n8, wc_p8)
-        for h in halves:
             nc.vector.scalar_tensor_tensor(flat(g[h]), flat(th[h]), 2.0, flat(rh[h]), ALU.mult, ALU.mult)
         red_x = [group_reduce("x%d" % h, x_bank[h]) for h in halves]
         for h in halves:
-            group_spread("x%d" % h, x_bank[h], red_x[h])
+            group_spread("x%d" % h, x_bank[h], red_x[h], nc.scalar.copy)
+        b = [new("b%d" % h, big, F32, "red_x%d" % h) for h in halves]
+        for h in halves:
+            per_tile(b[h], th2[h], wc_n8, wc_p8)
         for h in halves:
             nc.vector.tensor_tensor(flat(a[h]), flat(g[h]), flat(e[h]), ALU.add)
         for h in halves:
@@ -257,10 +261,12 @@ def tile_attend_hvpairbalance_kernel(tc, taba, dtab, tabb_words, tabb_scales, pw
             for t in range(JT):
                 turn(y_bank[h][:, t, :], up[h][:, t, :], False, t == JT - 1)
         for h in halves:
-            nc.vector.tensor_tensor(
-                y[h][:].rearrange("i (g t c) -> i g t c", t=JT, c=4),
-                y_bank[h][:].rearrange("i t (g c) -> i g t c", c=4),
-                base_sb[h][:].rearrange("i (g t c) -> i g t c", t=JT, c=4),
-                ALU.add,
-            )
-            nc.sync.dma_start(out[h * P : (h + 1) * P, :], y[h][:])
+            for part in range(2):
+                cols = slice(part * J // 2, (part + 1) * J // 2)
+                nc.vector.tensor_tensor(
+                    y[h][:, cols].rearrange("i (g t c) -> i g t c", t=JT, c=4),
+                    y_bank[h][:, :, part * P // 2 : (part + 1) * P // 2].rearrange("i t (g c) -> i g t c", c=4),
+                    base_sb[h][:, cols].rearrange("i (g t c) -> i g t c", t=JT, c=4),
+                    ALU.add,
+                )
+                nc.sync.dma_start(out[h * P : (h + 1) * P, cols], y[h][:, cols])

@@ -38,7 +38,6 @@ def tile_attend_hvpairbalance_kernel(tc, taba, dtab, tabb_words, tabb_scales, pw
         list_j = new("list_j", [P, J // 16], U16)
         words = new("words", [P, U], U16)
         scales = new("scales", [P, U], U8)
-        w16 = new("w16", [P, GROUP], F32)
         planes_a = [new("plane_a%d" % t, [P, T], F32) for t in range(PACK)]
         planes_d = [new("plane_d%d" % t, [P, T], F32) for t in range(PACK)]
         base_sb = [new("base%d" % h, [P, J], F32) for h in range(HALVES)]
@@ -50,10 +49,10 @@ def tile_attend_hvpairbalance_kernel(tc, taba, dtab, tabb_words, tabb_scales, pw
         nc.gpsimd.memset(warm[:], 0.0)
         nc.scalar.activation(warm_out[:], warm[:], ACT.Tanh)
         make_identity(nc, ident[:])
+        w16 = new("w16", [P, GROUP], F32)
 
         a_rows = taba.rearrange("(p t) c -> t p c", t=PACK)
         d_rows = dtab.rearrange("(p t) c -> t p c", t=PACK)
-        nc.gpsimd.dma_start(w16[:], pw.rearrange("o (g r) -> g o r", r=GROUP).to_broadcast([G, 4, GROUP]))
         nc.sync.dma_start(list_j[:], offs2)
         nc.sync.dma_start(words[:].bitcast(I32), tabb_words[0].bitcast(I32))
         for r in range(4):
@@ -61,6 +60,7 @@ def tile_attend_hvpairbalance_kernel(tc, taba, dtab, tabb_words, tabb_scales, pw
         nc.sync.dma_start(planes_a[0][:], a_rows[0])
         nc.sync.dma_start(planes_a[1][:], a_rows[1])
         nc.sync.dma_start(list_i[:], offs)
+        nc.sync.dma_start(w16[:], pw.rearrange("o (g r) -> g o r", r=GROUP).to_broadcast([G, 4, GROUP]))
         for t in range(2, PACK):
             nc.sync.dma_start(planes_a[t][:], a_rows[t])
         for t in range(PACK):
@@ -86,26 +86,27 @@ def tile_attend_hvpairbalance_kernel(tc, taba, dtab, tabb_words, tabb_scales, pw
             scales_g[:].bitcast(I32).rearrange("p (g t) -> p t g", t=JT),
         )
 
-        picked = new("picked", [P, JT, 4], F32, "words")
+        picked = new("picked", [P, JT, 4], F32)
+        paired = new("paired", [P, JT, 2], F32)
         w4 = new("w4", [P, JT], F32)
-        wsum = new("wsum", [P, 1], F32, "words_g")
+        wsum = new("wsum", [P, 1], F32)
+        w16_copy = new("w16_copy", [P, GROUP], F32)
         wmean_p8 = new("wmean_p8", [P, 1], F32)
         w_n8 = new("w_n8", [P, JT], F32)
         w_6 = new("w_6", [P, JT], F32)
         w_n2 = new("w_n2", [P, JT], F32)
         wc_n8 = new("wc_n8", [P, JT], F32)
-        wc_p8 = new("wc_p8", [P, JT], F32)
-        nc.vector.tensor_tensor(
+        nc.gpsimd.tensor_tensor(
             picked[:], w16[:].rearrange("p (t c) -> p t c", c=4), lane[:].unsqueeze(1).to_broadcast([P, JT, 4]), ALU.mult
         )
-        nc.vector.tensor_reduce(wsum[:], w16[:], AX.X, ALU.add)
-        nc.vector.tensor_reduce(w4[:], picked[:], AX.X, ALU.add)
+        nc.scalar.activation(w16_copy[:], w16[:], ACT.Copy, accum_out=wsum[:])
+        nc.gpsimd.tensor_tensor(paired[:], picked[:, :, 0:2], picked[:, :, 2:4], ALU.add)
+        nc.gpsimd.tensor_tensor(w4[:], paired[:, :, 0], paired[:, :, 1], ALU.add)
         nc.scalar.activation(wmean_p8[:], wsum[:], ACT.Copy, scale=0.125 / GROUP)
         nc.scalar.activation(w_n8[:], w4[:], ACT.Copy, scale=-0.125)
         nc.scalar.activation(wc_n8[:], w4[:], ACT.Identity, bias=wmean_p8[:], scale=-0.125)
         nc.scalar.activation(w_6[:], w4[:], ACT.Copy, scale=6.0)
         nc.scalar.activation(w_n2[:], w4[:], ACT.Copy, scale=-2.0)
-        nc.scalar.activation(wc_p8[:], wc_n8[:], ACT.Copy, scale=-1.0)
 
         def gather_woven(woven, planes, t):
             nc.vector.tensor_copy(woven[:, :, t], planes[t][:].indirect(list_i[:]))
@@ -236,9 +237,9 @@ def tile_attend_hvpairbalance_kernel(tc, taba, dtab, tabb_words, tabb_scales, pw
         red_x = [group_reduce("x%d" % h, x_bank[h]) for h in halves]
         for h in halves:
             group_spread("x%d" % h, x_bank[h], red_x[h], nc.scalar.copy)
-        b = [new("b%d" % h, big, F32, "red_x%d" % h) for h in halves]
+        px = [new("px%d" % h, [P, P], F32) for h in halves]
         for h in halves:
-            per_tile(b[h], th2[h], wc_n8, wc_p8)
+            nc.scalar.copy(px[h][:], x_bank[h][:, 3, :])
         for h in halves:
             nc.vector.tensor_tensor(flat(a[h]), flat(g[h]), flat(e[h]), ALU.add)
         for h in halves:
@@ -252,12 +253,14 @@ def tile_attend_hvpairbalance_kernel(tc, taba, dtab, tabb_words, tabb_scales, pw
             for t in range(JT):
                 turn(y_bank[h][:, t, :], z[h][:, t, :], t == 0, False)
         for h in halves:
-            nc.vector.tensor_tensor(bm[h][:], x_bank[h][:, 2:3, :].to_broadcast(big), b[h][:], ALU.mult)
-            nc.vector.scalar_tensor_tensor(
-                up[h][:], th2[h][:], 1.0, x_bank[h][:, 3:4, :].to_broadcast(big), ALU.subtract, ALU.mult
-            )
             for t in range(JT):
-                turn(y_bank[h][:, t, :], bm[h][:, t, :], False, False)
+                nc.vector.scalar_tensor_tensor(
+                    bm[h][:, t, :], x_bank[h][:, 2, :], wc_n8[:, t : t + 1], px[h][:], ALU.mult, ALU.add
+                )
+        for h in halves:
+            for pair in range(0, JT, 2):
+                two = slice(pair, pair + 2)
+                nc.vector.scalar_tensor_tensor(up[h][:, two, :], th2[h][:, two, :], 1.0, bm[h][:, two, :], ALU.subtract, ALU.mult)
             for t in range(JT):
                 turn(y_bank[h][:, t, :], up[h][:, t, :], False, t == JT - 1)
         for h in halves:

@@ -42,12 +42,8 @@ def tile_attend_hvpairbalance_kernel(tc, taba, dtab, tabb_words, tabb_scales, pw
         planes_d = [new("plane_d%d" % t, [P, T], F32) for t in range(PACK)]
         base_sb = [new("base%d" % h, [P, J], F32) for h in range(HALVES)]
         ident = new("ident", [P, P], F32)
-        warm = new("warm", [P, 1], F32)
-        warm_out = new("warm_out", [P, 1], F32)
 
         nc.vector.memset(scales[:].bitcast(I32), 0)
-        nc.gpsimd.memset(warm[:], 0.0)
-        nc.scalar.activation(warm_out[:], warm[:], ACT.Tanh)
         make_identity(nc, ident[:])
         w16 = new("w16", [P, GROUP], F32)
 
@@ -86,27 +82,25 @@ def tile_attend_hvpairbalance_kernel(tc, taba, dtab, tabb_words, tabb_scales, pw
             scales_g[:].bitcast(I32).rearrange("p (g t) -> p t g", t=JT),
         )
 
+        w16_n8 = new("w16_n8", [P, GROUP], F32)
+        wsum_n8 = new("wsum_n8", [P, 1], F32)
+        wmean_p8 = new("wmean_p8", [P, 1], F32)
         picked = new("picked", [P, JT, 4], F32)
         paired = new("paired", [P, JT, 2], F32)
-        w4 = new("w4", [P, JT], F32)
-        wsum = new("wsum", [P, 1], F32)
-        w16_copy = new("w16_copy", [P, GROUP], F32)
-        wmean_p8 = new("wmean_p8", [P, 1], F32)
         w_n8 = new("w_n8", [P, JT], F32)
+        wc_n8 = new("wc_n8", [P, JT], F32)
         w_6 = new("w_6", [P, JT], F32)
         w_n2 = new("w_n2", [P, JT], F32)
-        wc_n8 = new("wc_n8", [P, JT], F32)
+        nc.scalar.activation(w16_n8[:], w16[:], ACT.Copy, scale=-0.125, accum_out=wsum_n8[:])
         nc.gpsimd.tensor_tensor(
-            picked[:], w16[:].rearrange("p (t c) -> p t c", c=4), lane[:].unsqueeze(1).to_broadcast([P, JT, 4]), ALU.mult
+            picked[:], w16_n8[:].rearrange("p (t c) -> p t c", c=4), lane[:].unsqueeze(1).to_broadcast([P, JT, 4]), ALU.mult
         )
-        nc.scalar.activation(w16_copy[:], w16[:], ACT.Copy, accum_out=wsum[:])
         nc.gpsimd.tensor_tensor(paired[:], picked[:, :, 0:2], picked[:, :, 2:4], ALU.add)
-        nc.gpsimd.tensor_tensor(w4[:], paired[:, :, 0], paired[:, :, 1], ALU.add)
-        nc.scalar.activation(wmean_p8[:], wsum[:], ACT.Copy, scale=0.125 / GROUP)
-        nc.scalar.activation(w_n8[:], w4[:], ACT.Copy, scale=-0.125)
-        nc.scalar.activation(wc_n8[:], w4[:], ACT.Identity, bias=wmean_p8[:], scale=-0.125)
-        nc.scalar.activation(w_6[:], w4[:], ACT.Copy, scale=6.0)
-        nc.scalar.activation(w_n2[:], w4[:], ACT.Copy, scale=-2.0)
+        nc.gpsimd.tensor_tensor(w_n8[:], paired[:, :, 0], paired[:, :, 1], ALU.add)
+        nc.scalar.activation(wmean_p8[:], wsum_n8[:], ACT.Copy, scale=-1.0 / GROUP)
+        nc.scalar.activation(wc_n8[:], w_n8[:], ACT.Identity, bias=wmean_p8[:], scale=1.0)
+        nc.scalar.activation(w_6[:], w_n8[:], ACT.Copy, scale=-48.0)
+        nc.scalar.activation(w_n2[:], w_n8[:], ACT.Copy, scale=16.0)
 
         def gather_woven(woven, planes, t):
             nc.vector.tensor_copy(woven[:, :, t], planes[t][:].indirect(list_i[:]))
@@ -226,14 +220,14 @@ def tile_attend_hvpairbalance_kernel(tc, taba, dtab, tabb_words, tabb_scales, pw
             sum_over_tiles(x_bank[h][:, 0, :], x[h])
             sum_over_tiles(x_bank[h][:, 1, :], wx[h])
 
-        e = [new("e%d" % h, big, F32, "wx%d" % h) for h in halves]
+        e = [new("e%d" % h, big, F32, ("rep_h1", "wx0")[h]) for h in halves]
         g = [new("g%d" % h, big, F32) for h in halves]
-        a = [new("a%d" % h, big, F32) for h in halves]
+        a = [new("a%d" % h, big, F32, None) for h in halves]
         z = [new("z%d" % h, big, F32) for h in halves]
         for h in halves:
             per_tile(e[h], th2[h], w_6, w_n2)
         for h in halves:
-            nc.vector.scalar_tensor_tensor(flat(g[h]), flat(th[h]), 2.0, flat(rh[h]), ALU.mult, ALU.mult)
+            nc.gpsimd.tensor_tensor(flat(g[h]), flat(th[h]), flat(x[h]), ALU.mult)
         red_x = [group_reduce("x%d" % h, x_bank[h]) for h in halves]
         for h in halves:
             group_spread("x%d" % h, x_bank[h], red_x[h], nc.scalar.copy)
@@ -241,17 +235,17 @@ def tile_attend_hvpairbalance_kernel(tc, taba, dtab, tabb_words, tabb_scales, pw
         for h in halves:
             nc.scalar.copy(px[h][:], x_bank[h][:, 3, :])
         for h in halves:
-            nc.vector.tensor_tensor(flat(a[h]), flat(g[h]), flat(e[h]), ALU.add)
-        for h in halves:
-            nc.vector.tensor_tensor(flat(z[h]), flat(a[h]), flat(x[h]), ALU.mult)
+            nc.vector.scalar_tensor_tensor(flat(z[h]), flat(g[h]), 2.0, flat(rh[h]), ALU.mult, ALU.mult)
+            nc.vector.tensor_tensor(flat(a[h]), flat(e[h]), flat(x[h]), ALU.mult)
 
         bm = [new("bm%d" % h, big, F32) for h in halves]
         up = [new("up%d" % h, big, F32) for h in halves]
         y_bank = [ps.tile(big, F32, name="y%d" % h, tag="sy%d" % h) for h in halves]
         y = [new("yo%d" % h, [P, J], F32) for h in halves]
         for h in halves:
-            for t in range(JT):
-                turn(y_bank[h][:, t, :], z[h][:, t, :], t == 0, False)
+            for term in (z[h], a[h]):
+                for t in range(JT):
+                    turn(y_bank[h][:, t, :], term[:, t, :], term is z[h] and t == 0, False)
         for h in halves:
             for t in range(JT):
                 nc.vector.scalar_tensor_tensor(

from contextlib import ExitStack

import concourse.mybir as mybir
from concourse.masks import make_identity

D, T, U, I, J, G = 512, 1024, 1024, 256, 512, 32
FLOPS = 2 * 2 * D * I * J

F32 = mybir.dt.float32
BF16 = mybir.dt.bfloat16
I32 = mybir.dt.int32
U32 = mybir.dt.uint32
U16 = mybir.dt.uint16
U8 = mybir.dt.uint8
FP8X4 = mybir.dt.float8_e4m3fn_x4
FP4X4 = mybir.dt.float4_e2m1fn_x4
ALU = mybir.AluOpType
ACT = mybir.ActivationFunctionType
AX = mybir.AxisListType

P = 128
PACK = 4
HALVES = I // P
JT = J // P
GROUP = J // G


def tile_attend_hvpairbalance_kernel(tc, taba, dtab, tabb_words, tabb_scales, pw, base, offs, offs2, out):
    nc = tc.nc
    with ExitStack() as ctx:
        sb = ctx.enter_context(tc.tile_pool(name="sb", bufs=1))
        ps = ctx.enter_context(tc.psum_pool(name="ps", bufs=1))

        def new(name, shape, dtype, tag=None):
            return sb.tile(shape, dtype, name=name, tag=tag or name, align_bytes=64)

        list_i = new("list_i", [P, I // 16], U16)
        list_j = new("list_j", [P, J // 16], U16)
        words = new("words", [P, U], U16)
        scales = new("scales", [P, U], U8)
        planes_a = [new("plane_a%d" % t, [P, T], F32) for t in range(PACK)]
        planes_d = [new("plane_d%d" % t, [P, T], F32) for t in range(PACK)]
        base_sb = [new("base%d" % h, [P, J], F32) for h in range(HALVES)]
        ident = new("ident", [P, P], F32)

        nc.vector.memset(scales[:].bitcast(I32), 0)
        make_identity(nc, ident[:])
        w16 = new("w16", [P, GROUP], F32)

        a_rows = taba.rearrange("(p t) c -> t p c", t=PACK)
        d_rows = dtab.rearrange("(p t) c -> t p c", t=PACK)
        nc.sync.dma_start(list_j[:], offs2)
        nc.sync.dma_start(words[:].bitcast(I32), tabb_words[0].bitcast(I32))
        for r in range(4):
            nc.sync.dma_start(scales[r:P:32, :].bitcast(I32), tabb_scales[0, r:16:4, :].bitcast(I32))
        nc.sync.dma_start(planes_a[0][:], a_rows[0])
        nc.sync.dma_start(planes_a[1][:], a_rows[1])
        nc.sync.dma_start(list_i[:], offs)
        nc.sync.dma_start(w16[:], pw.rearrange("o (g r) -> g o r", r=GROUP).to_broadcast([G, 4, GROUP]))
        for t in range(2, PACK):
            nc.sync.dma_start(planes_a[t][:], a_rows[t])
        for t in range(PACK):
            nc.sync.dma_start(planes_d[t][:], d_rows[t])
        for h in range(HALVES):
            nc.sync.dma_start(base_sb[h][:], base[h * P : (h + 1) * P, :])

        lane = new("lane", [P, 4], F32)
        nc.vector.tensor_reduce(lane[:], ident[:].rearrange("p (a c) -> p c a", c=4), AX.X, ALU.add)

        words_g = new("words_g", [P, J], U16)
        scales_g = new("scales_g", [P, J], U8)
        words_t = new("words_t", [P, JT, P], U16)
        scales_t = new("scales_t", [P, JT, P], U8)
        nc.vector.tensor_copy(words_g[:], words[:].indirect(list_j[:]))
        nc.vector.tensor_copy(scales_g[:], scales[:].indirect(list_j[:]))
        nc.vector.tensor_copy(
            words_t[:].bitcast(I32).rearrange("p t (g e) -> p t g e", e=2),
            words_g[:].bitcast(I32).rearrange("p (g t e) -> p t g e", t=JT, e=2),
        )
        nc.vector.tensor_copy(
            scales_t[:].bitcast(I32),
            scales_g[:].bitcast(I32).rearrange("p (g t) -> p t g", t=JT),
        )

        w16_n8 = new("w16_n8", [P, GROUP], F32)
        wsum_n8 = new("wsum_n8", [P, 1], F32)
        wmean_p8 = new("wmean_p8", [P, 1], F32)
        picked = new("picked", [P, JT, 4], F32)
        paired = new("paired", [P, JT, 2], F32)
        w_n8 = new("w_n8", [P, JT], F32)
        wc_n8 = new("wc_n8", [P, JT], F32)
        w_6 = new("w_6", [P, JT], F32)
        w_n2 = new("w_n2", [P, JT], F32)
        nc.scalar.activation(w16_n8[:], w16[:], ACT.Copy, scale=-0.125, accum_out=wsum_n8[:])
        nc.gpsimd.tensor_tensor(
            picked[:], w16_n8[:].rearrange("p (t c) -> p t c", c=4), lane[:].unsqueeze(1).to_broadcast([P, JT, 4]), ALU.mult
        )
        nc.gpsimd.tensor_tensor(paired[:], picked[:, :, 0:2], picked[:, :, 2:4], ALU.add)
        nc.gpsimd.tensor_tensor(w_n8[:], paired[:, :, 0], paired[:, :, 1], ALU.add)
        nc.scalar.activation(wmean_p8[:], wsum_n8[:], ACT.Copy, scale=-1.0 / GROUP)
        nc.scalar.activation(wc_n8[:], w_n8[:], ACT.Identity, bias=wmean_p8[:], scale=1.0)
        nc.scalar.activation(w_6[:], w_n8[:], ACT.Copy, scale=-48.0)
        nc.scalar.activation(w_n2[:], w_n8[:], ACT.Copy, scale=16.0)

        def gather_woven(woven, planes, t):
            nc.vector.tensor_copy(woven[:, :, t], planes[t][:].indirect(list_i[:]))

        def gather_woven_half(woven, planes, t, h):
            cols = P // 16
            nc.vector.tensor_copy(woven[:, h * P : (h + 1) * P, t], planes[t][:].indirect(list_i[:, h * cols : (h + 1) * cols]))

        def quantize(name, woven, h):
            codes = new("codes_%s%d" % (name, h), [P, P], U32)
            plane = new("sc_%s%d" % (name, h), [P, P], U8)
            nc.vector.quantize_mx(
                out=codes[:].bitcast(FP8X4), scales=plane[:], in_=woven[:, h * P : (h + 1) * P, :].rearrange("p c t -> p (c t)")
            )
            return codes, plane

        def scores(bank, quantized):
            codes, plane = quantized
            for t in range(JT):
                nc.tensor.matmul_mx(
                    out=bank[:, t, :],
                    lhsT=words_t[:, t, :].bitcast(FP4X4),
                    lhsT_scale=scales_t[:, t, :],
                    rhs=codes[:].bitcast(FP8X4),
                    rhs_scale=plane[:],
                    start=True,
                    stop=True,
                )

        def turn(dst, src, start, stop):
            nc.tensor.matmul(dst, src, ident[:], start=start, stop=stop, is_transpose=True)

        def sum_over_tiles(dst, src):
            for t in range(JT):
                turn(dst, src[:, t, :], t == 0, t == JT - 1)

        def per_tile(dst, src, scale, bias=None):
            for t in range(JT):
                if bias is None:
                    nc.scalar.activation(dst[:, t, :], src[:, t, :], ACT.Copy, scale=scale[:, t : t + 1])
                else:
                    nc.scalar.activation(
                        dst[:, t, :], src[:, t, :], ACT.Identity, bias=bias[:, t : t + 1], scale=scale[:, t : t + 1]
                    )

        def group_reduce(name, bank, tag=None):
            red = new("red_" + name, [P, 2 * G, 1], F32, tag)
            nc.vector.tensor_reduce(red[:], bank[:, 0:2, :].rearrange("p q (g c) -> p (q g) c", c=4), AX.X, ALU.add)
            return red

        def group_spread(name, bank, red, copy):
            rep = new("rep_" + name, [P, 2 * G, 4], F32)
            copy(rep[:], red[:].to_broadcast([P, 2 * G, 4]))
            flat = rep[:].rearrange("p (q g) c -> p q (g c)", q=2)
            for q in range(2):
                turn(bank[:, 2 + q, :], flat[:, q, :], True, True)

        big = [P, JT, P]
        halves = range(HALVES)
        woven_a = new("woven_a", [P, I, PACK], BF16)
        woven_d = new("woven_d", [P, I, PACK], BF16)
        dense_a = new("dense_a", [P, 2, I], BF16)
        for t in range(2):
            nc.vector.tensor_copy(dense_a[:, t, :], planes_a[t][:].indirect(list_i[:]))
        nc.scalar.copy(woven_a[:, :, 0:2], dense_a[:].rearrange("p t c -> p c t"))
        gather_woven(woven_a, planes_a, 2)
        for h in halves:
            gather_woven_half(woven_a, planes_a, PACK - 1, h)
        quant_a = [quantize("a", woven_a, h) for h in halves]
        s_bank = [ps.tile(big, F32, name="s%d" % h, tag="sy%d" % h) for h in halves]
        for h in halves:
            scores(s_bank[h], quant_a[h])

        th = [new("th%d" % h, big, F32) for h in halves]
        wth = [new("wth%d" % h, big, F32) for h in halves]
        th2 = [new("thsq%d" % h, big, F32) for h in halves]
        h_bank = [ps.tile(big, F32, name="hb%d" % h) for h in halves]
        for h in halves:
            for pair in range(0, JT, 2):
                nc.scalar.activation(th[h][:, pair : pair + 2, :], s_bank[h][:, pair : pair + 2, :], ACT.Tanh)
            per_tile(wth[h], th[h], w_n8)
            sum_over_tiles(h_bank[h][:, 0, :], th[h])
            sum_over_tiles(h_bank[h][:, 1, :], wth[h])
        for h in halves:
            nc.scalar.activation(th2[h][:], th[h][:], ACT.Square)

        for t in range(PACK - 1):
            gather_woven(woven_d, planes_d, t)
        for h in halves:
            gather_woven_half(woven_d, planes_d, PACK - 1, h)
        quant_d = [quantize("d", woven_d, h) for h in halves]
        ts_bank = [ps.tile(big, F32, name="ts%d" % h) for h in halves]
        for h in halves:
            scores(ts_bank[h], quant_d[h])
        red_h = [group_reduce("h%d" % h, h_bank[h], ("plane_d3", "woven_d")[h]) for h in halves]
        for h in halves:
            group_spread("h%d" % h, h_bank[h], red_h[h], nc.scalar.copy)

        ph = [new("ph%d" % h, [P, P], F32) for h in halves]
        rh = [new("rh%d" % h, big, F32) for h in halves]
        for h in halves:
            nc.scalar.copy(ph[h][:], h_bank[h][:, 3, :])
            for t in range(JT):
                nc.vector.scalar_tensor_tensor(
                    rh[h][:, t, :], h_bank[h][:, 2, :], wc_n8[:, t : t + 1], ph[h][:], ALU.mult, ALU.add
                )

        def flat(x):
            return x[:].rearrange("p t i -> p (t i)")

        x = [new("x%d" % h, big, F32) for h in halves]
        wx = [new("wx%d" % h, big, F32) for h in halves]
        x_bank = [ps.tile(big, F32, name="xb%d" % h) for h in halves]
        for h in halves:
            nc.vector.scalar_tensor_tensor(flat(x[h]), flat(th2[h]), 1.0, flat(ts_bank[h]), ALU.subtract, ALU.mult)
            per_tile(wx[h], x[h], w_n8)
            sum_over_tiles(x_bank[h][:, 0, :], x[h])
            sum_over_tiles(x_bank[h][:, 1, :], wx[h])

        e = [new("e%d" % h, big, F32, ("rep_h1", "wx0")[h]) for h in halves]
        g = [new("g%d" % h, big, F32) for h in halves]
        a = [new("a%d" % h, big, F32, None) for h in halves]
        z = [new("z%d" % h, big, F32) for h in halves]
        for h in halves:
            per_tile(e[h], th2[h], w_6, w_n2)
        for h in halves:
            nc.gpsimd.tensor_tensor(flat(g[h]), flat(th[h]), flat(x[h]), ALU.mult)
        red_x = [group_reduce("x%d" % h, x_bank[h]) for h in halves]
        for h in halves:
            group_spread("x%d" % h, x_bank[h], red_x[h], nc.scalar.copy)
        px = [new("px%d" % h, [P, P], F32) for h in halves]
        for h in halves:
            nc.scalar.copy(px[h][:], x_bank[h][:, 3, :])
        for h in halves:
            nc.vector.scalar_tensor_tensor(flat(z[h]), flat(g[h]), 2.0, flat(rh[h]), ALU.mult, ALU.mult)
            nc.vector.tensor_tensor(flat(a[h]), flat(e[h]), flat(x[h]), ALU.mult)

        bm = [new("bm%d" % h, big, F32) for h in halves]
        up = [new("up%d" % h, big, F32) for h in halves]
        y_bank = [ps.tile(big, F32, name="y%d" % h, tag="sy%d" % h) for h in halves]
        y = [new("yo%d" % h, [P, J], F32) for h in halves]
        for h in halves:
            for term in (z[h], a[h]):
                for t in range(JT):
                    turn(y_bank[h][:, t, :], term[:, t, :], term is z[h] and t == 0, False)
        for h in halves:
            for t in range(JT):
                nc.vector.scalar_tensor_tensor(
                    bm[h][:, t, :], x_bank[h][:, 2, :], wc_n8[:, t : t + 1], px[h][:], ALU.mult, ALU.add
                )
        for h in halves:
            for pair in range(0, JT, 2):
                two = slice(pair, pair + 2)
                nc.vector.scalar_tensor_tensor(up[h][:, two, :], th2[h][:, two, :], 1.0, bm[h][:, two, :], ALU.subtract, ALU.mult)
            for t in range(JT):
                turn(y_bank[h][:, t, :], up[h][:, t, :], False, t == JT - 1)
        for h in halves:
            for part in range(2):
                cols = slice(part * J // 2, (part + 1) * J // 2)
                nc.vector.tensor_tensor(
                    y[h][:, cols].rearrange("i (g t c) -> i g t c", t=JT, c=4),
                    y_bank[h][:, :, part * P // 2 : (part + 1) * P // 2].rearrange("i t (g c) -> i g t c", c=4),
                    base_sb[h][:, cols].rearrange("i (g t c) -> i g t c", t=JT, c=4),
                    ALU.add,
                )
                nc.sync.dma_start(out[h * P : (h + 1) * P, cols], y[h][:, cols])
